import numpy as np
import ml_dtypes


def mxq(x, axis, fmt="e4m3"):
    dtype, down = {"e4m3": (ml_dtypes.float8_e4m3fn, 7), "e5m2": (ml_dtypes.float8_e5m2, 14)}[fmt]
    v = np.moveaxis(np.asarray(x, np.float32).astype(ml_dtypes.bfloat16).astype(np.float64), axis, -1)
    blocks = v.reshape(v.shape[:-1] + (-1, 32))
    amax = np.abs(blocks).max(-1, keepdims=True)
    byte = np.maximum(np.where(amax > 0, np.frexp(amax)[1] - 1 + 127, 0) - down, 1)
    scale = np.exp2(byte - 127.0)
    codes = (blocks / scale).astype(np.float32).astype(dtype).astype(np.float64)
    return np.moveaxis((codes * scale).reshape(v.shape), -1, axis)


WIDE = False


def mx_kscale(k):
    if not WIDE:
        return np.ones(k)
    levels = np.array([10, -10, 5, -5, 0])
    if k % 512:
        return np.exp2(np.random.permutation(np.resize(levels, k // 32))).repeat(32)
    a = np.empty((k // 512, 16))
    for p in range(k // 512):
        a[p, :8] = np.random.permutation(np.resize(levels, 8))
        for g in range(8):
            far = levels[np.abs(levels - a[p, g]) >= 10]
            a[p, g + 8] = far[np.random.randint(len(far))]
    return np.exp2(a.ravel()).repeat(32)


def f64(x):
    return np.asarray(x).astype(np.float64)


def striped8(idx):
    return np.concatenate([x.reshape(-1, 16).T for x in idx]).astype(np.uint16)


def runs(offs, k):
    lists = np.stack([offs[16 * r : 16 * r + 16].T.reshape(-1) for r in range(8)]).astype(np.int64)
    return lists[np.arange(k) % 512 // 64]


def pack_weight(w):
    k, n = w.shape
    w = f64(np.asarray(w, np.float32).astype(ml_dtypes.bfloat16)).reshape(k // 32, 32, n)
    amax = np.abs(w).max(1)
    byte = np.clip(np.where(amax > 0, np.frexp(amax)[1] - 1 + 127 - 7, 1), 1, 254)
    scaled = (w * np.exp2(127.0 - byte)[:, None, :]).reshape(k, n).astype(np.float32)
    words = np.ascontiguousarray(scaled.reshape(k // 512, 128, 4, n).transpose(0, 1, 3, 2)).astype(ml_dtypes.float8_e4m3fn).view(np.uint8)
    return words, np.ascontiguousarray(byte.astype(np.uint8).reshape(k // 512, 16, n))


def unpack_weight(words, scales):
    g, p, n, _ = words.shape
    vals = np.ascontiguousarray(words).view(ml_dtypes.float8_e4m3fn).astype(np.float64) * np.repeat(np.exp2(scales.astype(np.float64) - 127.0), 8, axis=1)[..., None]
    return vals.transpose(0, 1, 3, 2).reshape(g * 512, n)


E2M1 = np.array([0.0, 0.5, 1.0, 1.5, 2.0, 3.0, 4.0, 6.0, -0.0, -0.5, -1.0, -1.5, -2.0, -3.0, -4.0, -6.0])


def pack_fp4(w):
    k, n = w.shape
    w = f64(np.asarray(w, np.float32).astype(ml_dtypes.bfloat16)).reshape(k // 32, 32, n)
    amax = np.abs(w).max(1)
    mant, ex = np.frexp(amax / 6.0)
    byte = np.clip(np.where(amax > 0, np.where(mant > 0.5, ex, ex - 1) + 127, 1), 1, 254)
    scaled = (w * np.exp2(127.0 - byte)[:, None, :]).reshape(k, n).astype(np.float32)
    c = np.ascontiguousarray(scaled.reshape(k // 512, 128, 4, n).transpose(0, 1, 3, 2)).astype(ml_dtypes.float4_e2m1fn).view(np.uint8) & 0xF
    words = (c[..., 0::2] | (c[..., 1::2] << 4)).reshape(k // 512, 128, 2 * n)
    return np.ascontiguousarray(words), np.ascontiguousarray(byte.astype(np.uint8).reshape(k // 512, 16, n))


def unpack_fp4(words, scales):
    g, _, n = scales.shape
    words = np.ascontiguousarray(words).reshape(g, 128, n, 2)
    nib = np.empty((g, 128, n, 4), np.uint8)
    nib[..., 0::2] = words & 0xF
    nib[..., 1::2] = words >> 4
    vals = E2M1[nib] * np.repeat(np.exp2(scales.astype(np.float64) - 127.0), 8, axis=1)[..., None]
    return vals.transpose(0, 1, 3, 2).reshape(g * 512, n)


def planes(y):
    n, m = y.shape
    v = y.astype(np.float32).astype(ml_dtypes.bfloat16).astype(np.float64).reshape(n // 32, 32, m)
    top = np.abs(v).max(1)
    byte = np.clip(np.where(top > 0, np.frexp(top)[1] - 1 + 127 - 7, 1), 1, 254)
    codes = (v * np.exp2(127.0 - byte)[:, None, :]).reshape(n, m).astype(np.float32).astype(ml_dtypes.float8_e4m3fn).view(np.uint8)
    words = codes.reshape(n // 512, 128, 4, m).transpose(0, 1, 3, 2)
    return np.ascontiguousarray(words), np.ascontiguousarray(byte.astype(np.uint8).reshape(n // 512, 16, m))


K, T, S, H, C = 512, 2048, 512, 512, 512


def setup_inputs():
    n = np.random.standard_normal
    s = mx_kscale(K)[:, None]
    packed_xT = pack_weight(n((K, T)) * s)
    packed_w1 = pack_fp4(n((K, H)) / np.sqrt(K) / s)
    return {
        "x_words": packed_xT[0],
        "x_scales": packed_xT[1],
        "w1_words": packed_w1[0],
        "w1_scales": packed_w1[1],
        "gs": (np.random.uniform(0.5, 1.5, (K, 1)) / s).astype(np.float32),
        "offs": striped8(np.random.randint(0, T, (8, S))),
        "n1": striped8(np.stack([np.random.permutation(S) for _ in range(8)])),
        "n2": striped8(np.stack([np.random.permutation(S) for _ in range(8)])),
        "cand": striped8(np.random.randint(0, T, (8, C))),
        "n3": striped8(np.stack([np.random.permutation(S) for _ in range(8)])),
        "n4": striped8(np.stack([np.random.permutation(S) for _ in range(8)])),
    }


def reference(x_words, x_scales, w1_words, w1_scales, gs, offs, n1, n2, cand, n3, n4):
    x_cand = unpack_weight(x_words, x_scales)[np.arange(K)[:, None], runs(cand, K)]
    xq = unpack_weight(x_words, x_scales)[np.arange(K)[:, None], runs(offs, K)]
    y = unpack_fp4(w1_words, w1_scales).T @ xq
    st = y - (y[np.arange(H)[:, None], runs(n1, H)])
    z = f64(gs) * (st / (np.abs(st[np.arange(H)[:, None], runs(n2, H)]) + 0.5))
    s = 0.0625 * ((x_cand.T @ mxq(z, 0, "e4m3")))
    pa = s[np.arange(C)[:, None], runs(n3, C)]
    pb = s[np.arange(C)[:, None], runs(n4, C)]
    mu = 0.3125 * (s + pa + pb)
    out_0 = (s - mu) / (np.sqrt((pa - mu) ** 2 + (pb - mu) ** 2 + 0.25))
    return (out_0,) + planes(out_0)

@@ -1,0 +1,228 @@
+from contextlib import ExitStack
+
+import concourse.mybir as mybir
+
+K, T, S, H, C = 512, 2048, 512, 512, 512
+FLOPS = 2 * K * H * S + 2 * K * C * S
+
+F32 = mybir.dt.float32
+BF16 = mybir.dt.bfloat16
+I32 = mybir.dt.int32
+U32 = mybir.dt.uint32
+U16 = mybir.dt.uint16
+U8 = mybir.dt.uint8
+FP8X4 = mybir.dt.float8_e4m3fn_x4
+FP4X4 = mybir.dt.float4_e2m1fn_x4
+ALU = mybir.AluOpType
+ACT = mybir.ActivationFunctionType
+
+P = 128
+PACK = 4
+LANES = 16
+HALF = 256
+CHUNKS = ((0, 256), (256, 128), (384, 128))
+
+
+def tile_picked_hcandhopnstd_none_po_kernel(
+    tc, x_words, x_scales, w1_words, w1_scales, gs, offs, n1, n2, cand, n3, n4, out_0, out_1, out_2
+):
+    nc = tc.nc
+    with ExitStack() as ctx:
+        keep = ctx.enter_context(tc.tile_pool(name="keep", bufs=1))
+        psum = ctx.enter_context(tc.psum_pool(name="psum", bufs=1))
+
+        def load_list(name, dram):
+            tile = keep.tile([P, S // LANES], U16, name=name)
+            nc.sync.dma_start(tile[:], dram)
+            return tile
+
+        def entries(lst, c0, width):
+            return lst[:, c0 // LANES : (c0 + width) // LANES]
+
+        def interleave(copy, dst, src):
+            copy(
+                dst.rearrange("p (c i t) -> p c t i", i=4, t=PACK),
+                src.rearrange("p t (c i) -> p c t i", i=4),
+            )
+
+        x_sc = keep.tile([P, T], U8, name="x_sc")
+        nc.gpsimd.memset(x_sc[:].bitcast(I32), 0)
+        w_sc_raw = keep.tile([P, H], U8, name="w_sc_raw")
+        nc.gpsimd.memset(w_sc_raw[:].bitcast(I32), 0)
+
+        def load_w_scales(q):
+            nc.sync.dma_start(w_sc_raw[32 * q : 32 * q + 4, :].bitcast(I32), w1_scales[0, 4 * q : 4 * q + 4, :].bitcast(I32))
+
+        offs_t = load_list("offs_t", offs)
+        w_raw = keep.tile([P, 2 * H], U8, name="w_raw")
+        nc.sync.dma_start(w_raw[:].bitcast(I32), w1_words[0].bitcast(I32))
+        nc.sync.dma_start(x_sc[0:P:8, :].bitcast(I32), x_scales[0].bitcast(I32))
+        load_w_scales(0)
+        load_w_scales(1)
+        x_w = keep.tile([P, T], U32, name="x_w")
+        nc.sync.dma_start(x_w[:].bitcast(I32), x_words[0].rearrange("p n t -> p (n t)").bitcast(I32))
+        load_w_scales(2)
+        load_w_scales(3)
+        cand_t = load_list("cand_t", cand)
+        n1_t = load_list("n1_t", n1)
+        gs_t = keep.tile([P, PACK], F32, name="gs_t")
+        nc.sync.dma_start(gs_t[:], gs.rearrange("(p t) o -> p (t o)", t=PACK))
+        n2_t = load_list("n2_t", n2)
+        n3_t = load_list("n3_t", n3)
+        n4_t = load_list("n4_t", n4)
+
+        warm = keep.tile([P, 1], F32, name="warm")
+        nc.vector.memset(warm[:], 1.0)
+        nc.scalar.activation(warm[:], warm[:], ACT.Abs_reciprocal_sqrt)
+        xq_sc = keep.tile([P, S], U8, name="xq_sc", align_bytes=64)
+        xc_sc = keep.tile([P, C], U8, name="xc_sc", align_bytes=64)
+        nc.gpsimd.memset(xq_sc[:].bitcast(I32), 0)
+        nc.gpsimd.memset(xc_sc[:].bitcast(I32), 0)
+        win = [keep.tile([P, 2 * S], F32, name="win%d" % t) for t in range(PACK)]
+        for t in range(PACK):
+            nc.gpsimd.memset(win[t][:, S:], 0.0)
+        g_abs = keep.tile([P, PACK], F32, name="g_abs")
+        g_inv = keep.tile([P, PACK], F32, name="g_inv")
+        nc.scalar.activation(g_abs[:], gs_t[:], ACT.Abs)
+        nc.vector.tensor_scalar_max(g_abs[:], g_abs[:], 1e-30)
+        nc.vector.reciprocal(g_inv[:], g_abs[:])
+
+        def place_scales(dst, src):
+            for q in range(4):
+                nc.scalar.dma_start(dst[32 * q : 32 * q + 4, :].bitcast(I32), src[32 * q : 32 * q + 32 : 8, :].bitcast(I32))
+
+        xq_sc_g = keep.tile([P, S], U8, name="xq_sc_g")
+        nc.vector.tensor_copy(xq_sc_g[:], x_sc[:].indirect(offs_t[:]))
+        place_scales(xq_sc, xq_sc_g)
+
+        w_sc = keep.tile([P, H], U8, name="w_sc", align_bytes=64)
+        nc.vector.tensor_copy(
+            w_sc[:].rearrange("p (t m) -> p t m", t=PACK), w_sc_raw[:].rearrange("p (m t) -> p t m", t=PACK)
+        )
+        w_w = keep.tile([P, 2 * H], U8, name="w_w", align_bytes=64)
+        nc.vector.tensor_copy(
+            w_w[:].rearrange("p (t m b) -> p t m b", t=PACK, b=2),
+            w_raw[:].rearrange("p (m t b) -> p t m b", t=PACK, b=2),
+        )
+        xc_sc_g = keep.tile([P, C], U8, name="xc_sc_g")
+        nc.vector.tensor_copy(xc_sc_g[:], x_sc[:].indirect(cand_t[:]))
+        xc_sc_d = keep.tile([P, C], U8, name="xc_sc_d")
+        nc.vector.tensor_copy(
+            xc_sc_d[:].rearrange("p (t m) -> p t m", t=PACK), xc_sc_g[:].rearrange("p (m t) -> p t m", t=PACK)
+        )
+        place_scales(xc_sc, xc_sc_d)
+
+        xq_w = keep.tile([P, S], U32, name="xq_w", align_bytes=64)
+        nc.vector.tensor_copy(xq_w[:], x_w[:].indirect(offs_t[:]))
+
+        y_ps = [psum.tile([P, S], F32, name="y_ps%d" % t) for t in range(PACK)]
+        for t in range(PACK):
+            nc.tensor.matmul_mx(
+                y_ps[t][:],
+                lhsT=w_w[:, 2 * P * t : 2 * P * (t + 1)].bitcast(FP4X4),
+                lhsT_scale=w_sc[:, P * t : P * (t + 1)],
+                rhs=xq_w[:].bitcast(FP8X4),
+                rhs_scale=xq_sc[:],
+                start=True,
+                stop=True,
+            )
+
+        xc_w_g = keep.tile([P, C], U32, name="xc_w_g")
+        nc.vector.tensor_copy(xc_w_g[:], x_w[:].indirect(cand_t[:]))
+        xc_w = keep.tile([P, C], U32, name="xc_w", align_bytes=64)
+        nc.vector.tensor_copy(
+            xc_w[:].rearrange("p (t m) -> p t m", t=PACK), xc_w_g[:].rearrange("p (m t) -> p t m", t=PACK)
+        )
+
+        st, r = [], []
+        for t in range(PACK):
+            nc.scalar.activation(win[t][:, :S], y_ps[t][:], ACT.Copy, scale=gs_t[:, t : t + 1])
+            y_g = keep.tile([P, S], F32, name="y_g%d" % t)
+            nc.vector.tensor_copy(y_g[:], win[t][:].indirect(n1_t[:]))
+            st_t = keep.tile([P, S], F32, name="st%d" % t)
+            nc.vector.scalar_tensor_tensor(st_t[:], y_ps[t][:], gs_t[:, t : t + 1], y_g[:], ALU.mult, ALU.subtract)
+            mag = keep.tile([P, S], F32, name="mag%d" % t)
+            nc.scalar.activation(mag[:], st_t[:], ACT.Abs, scale=g_inv[:, t : t + 1])
+            root = keep.tile([P, S], F32, name="root%d" % t)
+            nc.scalar.activation(root[:], mag[:], ACT.Abs_reciprocal_sqrt, bias=0.5)
+            r_t = keep.tile([P, S], F32, name="r%d" % t)
+            nc.scalar.activation(r_t[:], root[:], ACT.Square)
+            st.append(st_t)
+            r.append(r_t)
+
+        z_w = keep.tile([P, S], U32, name="z_w", align_bytes=64)
+        z_sc = keep.tile([P, S], U8, name="z_sc", align_bytes=64)
+        s_ps = [psum.tile([P, S], F32, name="s_ps%d" % t) for t in range(PACK)]
+        for c0, width in CHUNKS:
+            cols = slice(c0, c0 + width)
+            z = keep.tile([P, PACK, width], F32, name="z%d" % c0)
+            for t in range(PACK):
+                nc.vector.tensor_tensor(z[:, t, :], r[t][:].indirect(entries(n2_t, c0, width)), st[t][:, cols], ALU.mult)
+            z_b = keep.tile([P, PACK * width], BF16, name="z_b%d" % c0, align_bytes=64)
+            interleave(nc.scalar.copy, z_b[:], z[:])
+            nc.vector.quantize_mx(z_w[:, cols].bitcast(FP8X4), z_sc[:, cols], z_b[:])
+            for t in range(PACK):
+                nc.tensor.matmul_mx(
+                    s_ps[t][:, cols],
+                    lhsT=xc_w[:, P * t : P * (t + 1)].bitcast(FP8X4),
+                    lhsT_scale=xc_sc[:, P * t : P * (t + 1)],
+                    rhs=z_w[:, cols].bitcast(FP8X4),
+                    rhs_scale=z_sc[:, cols],
+                    start=True,
+                    stop=True,
+                )
+            for t in range(PACK):
+                nc.scalar.activation(win[t][:, cols], s_ps[t][:, cols], ACT.Copy, scale=0.0625)
+
+        o_w = keep.tile([P, S], U32, name="o_w", align_bytes=64)
+        o_sc = keep.tile([P, S], U8, name="o_sc", align_bytes=64)
+        out_rows = out_0.rearrange("(p t) c -> p t c", t=PACK)
+        out_words = out_1[0].rearrange("p n t -> p (n t)").bitcast(I32)
+        o = keep.tile([P, PACK, S], F32, name="o")
+
+        def planes(name):
+            return [keep.tile([P, S], F32, name="%s%d" % (name, t)) for t in range(PACK)]
+
+        pa, u, v, w, num, v2, w2, q2, rs = [planes(name) for name in ("pa", "u", "v", "w", "num", "v2", "w2", "q2", "rs")]
+
+        def fetch_a(t):
+            nc.vector.tensor_copy(pa[t][:], win[t][:].indirect(n3_t[:]))
+
+        def fetch_b(t):
+            nc.vector.tensor_tensor(u[t][:], win[t][:].indirect(n4_t[:]), pa[t][:], ALU.add)
+
+        def forms(t):
+            nc.vector.scalar_tensor_tensor(v[t][:], pa[t][:], 2.0, u[t][:], ALU.mult, ALU.subtract)
+            nc.scalar.activation(v2[t][:], v[t][:], ACT.Square)
+            nc.vector.scalar_tensor_tensor(w[t][:], s_ps[t][:], 5.0 / 48.0, u[t][:], ALU.mult, ALU.subtract)
+            nc.scalar.activation(w2[t][:], w[t][:], ACT.Square, scale=0.375)
+            nc.vector.scalar_tensor_tensor(num[t][:], s_ps[t][:], 11.0 / 80.0, u[t][:], ALU.mult, ALU.subtract)
+
+        def spread(t):
+            nc.vector.tensor_tensor(q2[t][:], v2[t][:], w2[t][:], ALU.add)
+            nc.scalar.activation(rs[t][:], q2[t][:], ACT.Abs_reciprocal_sqrt, scale=0.5, bias=0.25)
+
+        def finish(t):
+            nc.vector.scalar_tensor_tensor(o[:, t, :], num[t][:], 0.3125, rs[t][:], ALU.mult, ALU.mult)
+            nc.sync.dma_start(out_rows[:, t, :], o[:, t, :])
+
+        for t in range(PACK):
+            fetch_a(t)
+            if t >= 1:
+                spread(t - 1)
+            fetch_b(t)
+            if t >= 2:
+                finish(t - 2)
+            forms(t)
+        spread(PACK - 1)
+        finish(PACK - 2)
+        finish(PACK - 1)
+
+        for c0, copy in ((0, nc.vector.tensor_copy), (HALF, nc.scalar.copy)):
+            cols = slice(c0, c0 + HALF)
+            o_b = keep.tile([P, PACK * HALF], BF16, name="o_b%d" % c0, align_bytes=64)
+            interleave(copy, o_b[:], o[:, :, cols])
+            nc.vector.quantize_mx(o_w[:, cols].bitcast(FP8X4), o_sc[:, cols], o_b[:])
+            nc.sync.dma_start(out_words[:, cols], o_w[:, cols].bitcast(I32))
+        for q in range(4):
+            nc.scalar.dma_start(out_2[0, 4 * q : 4 * q + 4, :].bitcast(I32), o_sc[32 * q : 32 * q + 4, :].bitcast(I32))

@@ -1,6 +1,7 @@
 from contextlib import ExitStack
 
 import concourse.mybir as mybir
+from concourse.masks import make_identity
 
 K, T, S, H, C = 512, 2048, 512, 512, 512
 FLOPS = 2 * K * H * S + 2 * K * C * S
@@ -20,7 +21,7 @@ P = 128
 PACK = 4
 LANES = 16
 HALF = 256
-CHUNKS = ((0, 256), (256, 128), (384, 128))
+CHUNKS = ((0, 256), (256, 256))
 
 
 def tile_picked_hcandhopnstd_none_po_kernel(
@@ -46,27 +47,26 @@ def tile_picked_hcandhopnstd_none_po_kernel(
             )
 
         x_sc = keep.tile([P, T], U8, name="x_sc")
-        nc.gpsimd.memset(x_sc[:].bitcast(I32), 0)
         w_sc_raw = keep.tile([P, H], U8, name="w_sc_raw")
-        nc.gpsimd.memset(w_sc_raw[:].bitcast(I32), 0)
 
         def load_w_scales(q):
-            nc.sync.dma_start(w_sc_raw[32 * q : 32 * q + 4, :].bitcast(I32), w1_scales[0, 4 * q : 4 * q + 4, :].bitcast(I32))
+            rows = w1_scales[0, 4 * q : 4 * q + 4, :].bitcast(I32)
+            nc.sync.dma_start(w_sc_raw[32 * q : 32 * q + 32, :].bitcast(I32), rows.unsqueeze(0).to_broadcast([8, 4, H // 4]))
 
         offs_t = load_list("offs_t", offs)
+        nc.sync.dma_start(x_sc[:].bitcast(I32), x_scales[0].bitcast(I32).unsqueeze(1).to_broadcast([16, 8, T // 4]))
         w_raw = keep.tile([P, 2 * H], U8, name="w_raw")
         nc.sync.dma_start(w_raw[:].bitcast(I32), w1_words[0].bitcast(I32))
-        nc.sync.dma_start(x_sc[0:P:8, :].bitcast(I32), x_scales[0].bitcast(I32))
         load_w_scales(0)
         load_w_scales(1)
+        load_w_scales(2)
         x_w = keep.tile([P, T], U32, name="x_w")
         nc.sync.dma_start(x_w[:].bitcast(I32), x_words[0].rearrange("p n t -> p (n t)").bitcast(I32))
-        load_w_scales(2)
         load_w_scales(3)
         cand_t = load_list("cand_t", cand)
-        n1_t = load_list("n1_t", n1)
         gs_t = keep.tile([P, PACK], F32, name="gs_t")
         nc.sync.dma_start(gs_t[:], gs.rearrange("(p t) o -> p (t o)", t=PACK))
+        n1_t = load_list("n1_t", n1)
         n2_t = load_list("n2_t", n2)
         n3_t = load_list("n3_t", n3)
         n4_t = load_list("n4_t", n4)
@@ -81,28 +81,30 @@ def tile_picked_hcandhopnstd_none_po_kernel(
         win = [keep.tile([P, 2 * S], F32, name="win%d" % t) for t in range(PACK)]
         for t in range(PACK):
             nc.gpsimd.memset(win[t][:, S:], 0.0)
+        ident = keep.tile([P, P], F32, name="ident")
+        make_identity(nc, ident[:])
         g_abs = keep.tile([P, PACK], F32, name="g_abs")
         g_inv = keep.tile([P, PACK], F32, name="g_inv")
         nc.scalar.activation(g_abs[:], gs_t[:], ACT.Abs)
         nc.vector.tensor_scalar_max(g_abs[:], g_abs[:], 1e-30)
         nc.vector.reciprocal(g_inv[:], g_abs[:])
 
-        def place_scales(dst, src):
+        def place_scales(queue, dst, src):
             for q in range(4):
-                nc.scalar.dma_start(dst[32 * q : 32 * q + 4, :].bitcast(I32), src[32 * q : 32 * q + 32 : 8, :].bitcast(I32))
+                queue.dma_start(dst[32 * q : 32 * q + 4, :].bitcast(I32), src[32 * q : 32 * q + 32 : 8, :].bitcast(I32))
 
         xq_sc_g = keep.tile([P, S], U8, name="xq_sc_g")
         nc.vector.tensor_copy(xq_sc_g[:], x_sc[:].indirect(offs_t[:]))
-        place_scales(xq_sc, xq_sc_g)
+        place_scales(nc.scalar, xq_sc, xq_sc_g)
 
-        w_sc = keep.tile([P, H], U8, name="w_sc", align_bytes=64)
-        nc.vector.tensor_copy(
-            w_sc[:].rearrange("p (t m) -> p t m", t=PACK), w_sc_raw[:].rearrange("p (m t) -> p t m", t=PACK)
-        )
         w_w = keep.tile([P, 2 * H], U8, name="w_w", align_bytes=64)
-        nc.vector.tensor_copy(
+        nc.gpsimd.tensor_copy(
             w_w[:].rearrange("p (t m b) -> p t m b", t=PACK, b=2),
             w_raw[:].rearrange("p (m t b) -> p t m b", t=PACK, b=2),
+        )
+        w_sc = keep.tile([P, H], U8, name="w_sc", align_bytes=64)
+        nc.gpsimd.tensor_copy(
+            w_sc[:].rearrange("p (t m) -> p t m", t=PACK), w_sc_raw[:].rearrange("p (m t) -> p t m", t=PACK)
         )
         xc_sc_g = keep.tile([P, C], U8, name="xc_sc_g")
         nc.vector.tensor_copy(xc_sc_g[:], x_sc[:].indirect(cand_t[:]))
@@ -110,12 +112,12 @@ def tile_picked_hcandhopnstd_none_po_kernel(
         nc.vector.tensor_copy(
             xc_sc_d[:].rearrange("p (t m) -> p t m", t=PACK), xc_sc_g[:].rearrange("p (m t) -> p t m", t=PACK)
         )
-        place_scales(xc_sc, xc_sc_d)
+        place_scales(nc.sync, xc_sc, xc_sc_d)
 
         xq_w = keep.tile([P, S], U32, name="xq_w", align_bytes=64)
         nc.vector.tensor_copy(xq_w[:], x_w[:].indirect(offs_t[:]))
 
-        y_ps = [psum.tile([P, S], F32, name="y_ps%d" % t) for t in range(PACK)]
+        y_ps = [psum.tile([P, S], F32, name="y_ps%d" % t, tag="y", bufs=PACK) for t in range(PACK)]
         for t in range(PACK):
             nc.tensor.matmul_mx(
                 y_ps[t][:],
@@ -134,91 +136,117 @@ def tile_picked_hcandhopnstd_none_po_kernel(
             xc_w[:].rearrange("p (t m) -> p t m", t=PACK), xc_w_g[:].rearrange("p (m t) -> p t m", t=PACK)
         )
 
-        st, r = [], []
-        for t in range(PACK):
+        def planes(name):
+            return [keep.tile([P, S], F32, name="%s%d" % (name, t)) for t in range(PACK)]
+
+        y_g, st, mag, root, r = [planes(name) for name in ("y_g", "st", "mag", "root", "r")]
+
+        def leave(t):
             nc.scalar.activation(win[t][:, :S], y_ps[t][:], ACT.Copy, scale=gs_t[:, t : t + 1])
-            y_g = keep.tile([P, S], F32, name="y_g%d" % t)
-            nc.vector.tensor_copy(y_g[:], win[t][:].indirect(n1_t[:]))
-            st_t = keep.tile([P, S], F32, name="st%d" % t)
-            nc.vector.scalar_tensor_tensor(st_t[:], y_ps[t][:], gs_t[:, t : t + 1], y_g[:], ALU.mult, ALU.subtract)
-            mag = keep.tile([P, S], F32, name="mag%d" % t)
-            nc.scalar.activation(mag[:], st_t[:], ACT.Abs, scale=g_inv[:, t : t + 1])
-            root = keep.tile([P, S], F32, name="root%d" % t)
-            nc.scalar.activation(root[:], mag[:], ACT.Abs_reciprocal_sqrt, bias=0.5)
-            r_t = keep.tile([P, S], F32, name="r%d" % t)
-            nc.scalar.activation(r_t[:], root[:], ACT.Square)
-            st.append(st_t)
-            r.append(r_t)
+
+        def differ(t):
+            nc.vector.tensor_copy(y_g[t][:], win[t][:].indirect(n1_t[:]))
+            nc.vector.scalar_tensor_tensor(st[t][:], y_ps[t][:], gs_t[:, t : t + 1], y_g[t][:], ALU.mult, ALU.subtract)
+
+        def size(t):
+            nc.scalar.activation(mag[t][:], st[t][:], ACT.Abs, scale=g_inv[:, t : t + 1])
+
+        def inv_root(t):
+            nc.scalar.activation(root[t][:], mag[t][:], ACT.Abs_reciprocal_sqrt, bias=0.5)
+
+        def square(t):
+            nc.scalar.activation(r[t][:], root[t][:], ACT.Square)
+
+        for t in range(PACK):
+            leave(t)
+        for t in range(PACK):
+            differ(t)
+            size(t)
+            if t > 0:
+                square(t - 1)
+            inv_root(t)
+        square(PACK - 1)
 
         z_w = keep.tile([P, S], U32, name="z_w", align_bytes=64)
         z_sc = keep.tile([P, S], U8, name="z_sc", align_bytes=64)
-        s_ps = [psum.tile([P, S], F32, name="s_ps%d" % t) for t in range(PACK)]
-        for c0, width in CHUNKS:
-            cols = slice(c0, c0 + width)
-            z = keep.tile([P, PACK, width], F32, name="z%d" % c0)
-            for t in range(PACK):
-                nc.vector.tensor_tensor(z[:, t, :], r[t][:].indirect(entries(n2_t, c0, width)), st[t][:, cols], ALU.mult)
-            z_b = keep.tile([P, PACK * width], BF16, name="z_b%d" % c0, align_bytes=64)
-            interleave(nc.scalar.copy, z_b[:], z[:])
-            nc.vector.quantize_mx(z_w[:, cols].bitcast(FP8X4), z_sc[:, cols], z_b[:])
-            for t in range(PACK):
-                nc.tensor.matmul_mx(
-                    s_ps[t][:, cols],
-                    lhsT=xc_w[:, P * t : P * (t + 1)].bitcast(FP8X4),
-                    lhsT_scale=xc_sc[:, P * t : P * (t + 1)],
-                    rhs=z_w[:, cols].bitcast(FP8X4),
-                    rhs_scale=z_sc[:, cols],
-                    start=True,
-                    stop=True,
-                )
-            for t in range(PACK):
-                nc.scalar.activation(win[t][:, cols], s_ps[t][:, cols], ACT.Copy, scale=0.0625)
+        s_ps = [psum.tile([P, S], F32, name="s_ps%d" % t, tag="s", bufs=PACK) for t in range(PACK)]
+        z = [keep.tile([P, PACK, width], F32, name="z%d" % c0) for c0, width in CHUNKS]
+
+        def weigh(chunk, t):
+            c0, width = CHUNKS[chunk]
+            nc.vector.tensor_tensor(
+                z[chunk][:, t, :], r[t][:].indirect(entries(n2_t, c0, width)), st[t][:, c0 : c0 + width], ALU.mult
+            )
+
+        for t in range(PACK):
+            for chunk in range(len(CHUNKS)):
+                weigh(chunk, t)
+        z_b = [keep.tile([P, PACK * width], BF16, name="z_b%d" % c0, align_bytes=64) for c0, width in CHUNKS]
+        interleave(nc.scalar.copy, z_b[0][:], z[0][:])
+        interleave(nc.vector.tensor_copy, z_b[1][:], z[1][:])
+        for chunk in (1, 0):
+            cols = slice(CHUNKS[chunk][0], sum(CHUNKS[chunk]))
+            nc.vector.quantize_mx(z_w[:, cols].bitcast(FP8X4), z_sc[:, cols], z_b[chunk][:])
+        for t in range(PACK):
+            nc.tensor.matmul_mx(
+                s_ps[t][:],
+                lhsT=xc_w[:, P * t : P * (t + 1)].bitcast(FP8X4),
+                lhsT_scale=xc_sc[:, P * t : P * (t + 1)],
+                rhs=z_w[:].bitcast(FP8X4),
+                rhs_scale=z_sc[:],
+                start=True,
+                stop=True,
+            )
+        nc.scalar.activation(win[0][:, :S], s_ps[0][:], ACT.Copy, scale=0.0625)
 
         o_w = keep.tile([P, S], U32, name="o_w", align_bytes=64)
         o_sc = keep.tile([P, S], U8, name="o_sc", align_bytes=64)
         out_rows = out_0.rearrange("(p t) c -> p t c", t=PACK)
         out_words = out_1[0].rearrange("p n t -> p (n t)").bitcast(I32)
         o = keep.tile([P, PACK, S], F32, name="o")
+        pa, u, v, s3, num, v2, w2, rs = [planes(name) for name in ("pa", "u", "v", "s3", "num", "v2", "w2", "rs")]
 
-        def planes(name):
-            return [keep.tile([P, S], F32, name="%s%d" % (name, t)) for t in range(PACK)]
-
-        pa, u, v, w, num, v2, w2, q2, rs = [planes(name) for name in ("pa", "u", "v", "w", "num", "v2", "w2", "q2", "rs")]
-
-        def fetch_a(t):
-            nc.vector.tensor_copy(pa[t][:], win[t][:].indirect(n3_t[:]))
-
-        def fetch_b(t):
-            nc.vector.tensor_tensor(u[t][:], win[t][:].indirect(n4_t[:]), pa[t][:], ALU.add)
-
-        def forms(t):
-            nc.vector.scalar_tensor_tensor(v[t][:], pa[t][:], 2.0, u[t][:], ALU.mult, ALU.subtract)
-            nc.scalar.activation(v2[t][:], v[t][:], ACT.Square)
-            nc.vector.scalar_tensor_tensor(w[t][:], s_ps[t][:], 5.0 / 48.0, u[t][:], ALU.mult, ALU.subtract)
-            nc.scalar.activation(w2[t][:], w[t][:], ACT.Square, scale=0.375)
-            nc.vector.scalar_tensor_tensor(num[t][:], s_ps[t][:], 11.0 / 80.0, u[t][:], ALU.mult, ALU.subtract)
-
-        def spread(t):
-            nc.vector.tensor_tensor(q2[t][:], v2[t][:], w2[t][:], ALU.add)
-            nc.scalar.activation(rs[t][:], q2[t][:], ACT.Abs_reciprocal_sqrt, scale=0.5, bias=0.25)
-
-        def finish(t):
-            nc.vector.scalar_tensor_tensor(o[:, t, :], num[t][:], 0.3125, rs[t][:], ALU.mult, ALU.mult)
-            nc.sync.dma_start(out_rows[:, t, :], o[:, t, :])
+        def turned_sum(bank, terms):
+            for c0 in range(0, S, P):
+                for i, term in enumerate(terms):
+                    nc.tensor.matmul(
+                        bank[:, c0 : c0 + P],
+                        term[:, c0 : c0 + P],
+                        ident[:],
+                        start=(i == 0),
+                        stop=(i == len(terms) - 1),
+                        is_transpose=True,
+                    )
 
         for t in range(PACK):
-            fetch_a(t)
-            if t >= 1:
-                spread(t - 1)
-            fetch_b(t)
-            if t >= 2:
-                finish(t - 2)
-            forms(t)
-        spread(PACK - 1)
-        finish(PACK - 2)
-        finish(PACK - 1)
+            if t + 1 < PACK:
+                nc.scalar.activation(win[t + 1][:, :S], s_ps[t + 1][:], ACT.Copy, scale=0.0625)
+            nc.scalar.activation(s3[t][:], s_ps[t][:], ACT.Copy, scale=-5.0 / 48.0)
+            nc.vector.tensor_copy(pa[t][:], win[t][:].indirect(n3_t[:]))
+            nc.vector.tensor_tensor(v[t][:], win[t][:].indirect(n4_t[:]), pa[t][:], ALU.subtract)
+            nc.vector.scalar_tensor_tensor(u[t][:], pa[t][:], 2.0, v[t][:], ALU.mult, ALU.add)
+            v_ps = psum.tile([P, S], F32, name="v_ps%d" % t, tag="y", bufs=PACK)
+            turned_sum(v_ps, (v[t],))
+            nc.scalar.activation(v2[t][:], v_ps[:], ACT.Square)
+            w_ps = psum.tile([P, S], F32, name="w_ps%d" % t, tag="y", bufs=PACK)
+            turned_sum(w_ps, (s3[t], u[t]))
+            nc.scalar.activation(w2[t][:], w_ps[:], ACT.Square, scale=0.375)
+            q_ps = psum.tile([P, S], F32, name="q_ps%d" % t, tag="s", bufs=PACK)
+            turned_sum(q_ps, (v2[t], w2[t]))
+            nc.scalar.activation(rs[t][:], q_ps[:], ACT.Abs_reciprocal_sqrt, scale=0.5, bias=0.25)
 
-        for c0, copy in ((0, nc.vector.tensor_copy), (HALF, nc.scalar.copy)):
+        for t in range(PACK):
+            nc.vector.scalar_tensor_tensor(num[t][:], win[t][:, :S], 2.2, u[t][:], ALU.mult, ALU.subtract)
+        last = PACK - 1
+        for t in range(last):
+            nc.vector.scalar_tensor_tensor(o[:, t, :], num[t][:], 0.3125, rs[t][:], ALU.mult, ALU.mult)
+            nc.sync.dma_start(out_rows[:, t, :], o[:, t, :])
+        halves = ((0, nc.scalar.copy), (HALF, nc.vector.tensor_copy))
+        for c0, copy in halves:
+            cols = slice(c0, c0 + HALF)
+            nc.vector.scalar_tensor_tensor(o[:, last, cols], num[last][:, cols], 0.3125, rs[last][:, cols], ALU.mult, ALU.mult)
+        nc.sync.dma_start(out_rows[:, last, :], o[:, last, :])
+        for c0, copy in reversed(halves):
             cols = slice(c0, c0 + HALF)
             o_b = keep.tile([P, PACK * HALF], BF16, name="o_b%d" % c0, align_bytes=64)
             interleave(copy, o_b[:], o[:, :, cols])

@@ -57,13 +57,13 @@ def tile_picked_hcandhopnstd_none_po_kernel(
         nc.sync.dma_start(x_sc[:].bitcast(I32), x_scales[0].bitcast(I32).unsqueeze(1).to_broadcast([16, 8, T // 4]))
         w_raw = keep.tile([P, 2 * H], U8, name="w_raw")
         nc.sync.dma_start(w_raw[:].bitcast(I32), w1_words[0].bitcast(I32))
+        cand_t = load_list("cand_t", cand)
         load_w_scales(0)
         load_w_scales(1)
-        load_w_scales(2)
         x_w = keep.tile([P, T], U32, name="x_w")
         nc.sync.dma_start(x_w[:].bitcast(I32), x_words[0].rearrange("p n t -> p (n t)").bitcast(I32))
+        load_w_scales(2)
         load_w_scales(3)
-        cand_t = load_list("cand_t", cand)
         gs_t = keep.tile([P, PACK], F32, name="gs_t")
         nc.sync.dma_start(gs_t[:], gs.rearrange("(p t) o -> p (t o)", t=PACK))
         n1_t = load_list("n1_t", n1)
@@ -85,9 +85,8 @@ def tile_picked_hcandhopnstd_none_po_kernel(
         make_identity(nc, ident[:])
         g_abs = keep.tile([P, PACK], F32, name="g_abs")
         g_inv = keep.tile([P, PACK], F32, name="g_inv")
-        nc.scalar.activation(g_abs[:], gs_t[:], ACT.Abs)
-        nc.vector.tensor_scalar_max(g_abs[:], g_abs[:], 1e-30)
-        nc.vector.reciprocal(g_inv[:], g_abs[:])
+        nc.scalar.activation(g_abs[:], gs_t[:], ACT.Abs_reciprocal_sqrt, bias=1e-30)
+        nc.scalar.activation(g_inv[:], g_abs[:], ACT.Square)
 
         def place_scales(queue, dst, src):
             for q in range(4):
@@ -117,7 +116,7 @@ def tile_picked_hcandhopnstd_none_po_kernel(
         xq_w = keep.tile([P, S], U32, name="xq_w", align_bytes=64)
         nc.vector.tensor_copy(xq_w[:], x_w[:].indirect(offs_t[:]))
 
-        y_ps = [psum.tile([P, S], F32, name="y_ps%d" % t, tag="y", bufs=PACK) for t in range(PACK)]
+        y_ps = [psum.tile([P, S], F32, name="y_ps%d" % t, tag="y%d" % t) for t in range(PACK)]
         for t in range(PACK):
             nc.tensor.matmul_mx(
                 y_ps[t][:],
@@ -146,7 +145,7 @@ def tile_picked_hcandhopnstd_none_po_kernel(
 
         def differ(t):
             nc.vector.tensor_copy(y_g[t][:], win[t][:].indirect(n1_t[:]))
-            nc.vector.scalar_tensor_tensor(st[t][:], y_ps[t][:], gs_t[:, t : t + 1], y_g[t][:], ALU.mult, ALU.subtract)
+            nc.gpsimd.tensor_tensor(st[t][:], win[t][:, :S], y_g[t][:], ALU.subtract)
 
         def size(t):
             nc.scalar.activation(mag[t][:], st[t][:], ACT.Abs, scale=g_inv[:, t : t + 1])
@@ -169,7 +168,7 @@ def tile_picked_hcandhopnstd_none_po_kernel(
 
         z_w = keep.tile([P, S], U32, name="z_w", align_bytes=64)
         z_sc = keep.tile([P, S], U8, name="z_sc", align_bytes=64)
-        s_ps = [psum.tile([P, S], F32, name="s_ps%d" % t, tag="s", bufs=PACK) for t in range(PACK)]
+        s_ps = [psum.tile([P, S], F32, name="s_ps%d" % t, tag="s%d" % t) for t in range(PACK)]
         z = [keep.tile([P, PACK, width], F32, name="z%d" % c0) for c0, width in CHUNKS]
 
         def weigh(chunk, t):
@@ -218,6 +217,11 @@ def tile_picked_hcandhopnstd_none_po_kernel(
                         is_transpose=True,
                     )
 
+        def spread(t):
+            q_ps = psum.tile([P, S], F32, name="q_ps%d" % t, tag="y%d" % ((t + 1) % PACK))
+            turned_sum(q_ps, (v2[t], w2[t]))
+            nc.scalar.activation(rs[t][:], q_ps[:], ACT.Abs_reciprocal_sqrt, scale=0.5, bias=0.25)
+
         for t in range(PACK):
             if t + 1 < PACK:
                 nc.scalar.activation(win[t + 1][:, :S], s_ps[t + 1][:], ACT.Copy, scale=0.0625)
@@ -225,15 +229,15 @@ def tile_picked_hcandhopnstd_none_po_kernel(
             nc.vector.tensor_copy(pa[t][:], win[t][:].indirect(n3_t[:]))
             nc.vector.tensor_tensor(v[t][:], win[t][:].indirect(n4_t[:]), pa[t][:], ALU.subtract)
             nc.vector.scalar_tensor_tensor(u[t][:], pa[t][:], 2.0, v[t][:], ALU.mult, ALU.add)
-            v_ps = psum.tile([P, S], F32, name="v_ps%d" % t, tag="y", bufs=PACK)
+            v_ps = psum.tile([P, S], F32, name="v_ps%d" % t, tag="y%d" % t)
             turned_sum(v_ps, (v[t],))
             nc.scalar.activation(v2[t][:], v_ps[:], ACT.Square)
-            w_ps = psum.tile([P, S], F32, name="w_ps%d" % t, tag="y", bufs=PACK)
+            w_ps = psum.tile([P, S], F32, name="w_ps%d" % t, tag="s%d" % t)
             turned_sum(w_ps, (s3[t], u[t]))
             nc.scalar.activation(w2[t][:], w_ps[:], ACT.Square, scale=0.375)
-            q_ps = psum.tile([P, S], F32, name="q_ps%d" % t, tag="s", bufs=PACK)
-            turned_sum(q_ps, (v2[t], w2[t]))
-            nc.scalar.activation(rs[t][:], q_ps[:], ACT.Abs_reciprocal_sqrt, scale=0.5, bias=0.25)
+            if t > 0:
+                spread(t - 1)
+        spread(PACK - 1)
 
         for t in range(PACK):
             nc.vector.scalar_tensor_tensor(num[t][:], win[t][:, :S], 2.2, u[t][:], ALU.mult, ALU.subtract)

@@ -21,7 +21,7 @@ P = 128
 PACK = 4
 LANES = 16
 HALF = 256
-CHUNKS = ((0, 256), (256, 256))
+CHUNK = 128
 
 
 def tile_picked_hcandhopnstd_none_po_kernel(
@@ -57,13 +57,13 @@ def tile_picked_hcandhopnstd_none_po_kernel(
         nc.sync.dma_start(x_sc[:].bitcast(I32), x_scales[0].bitcast(I32).unsqueeze(1).to_broadcast([16, 8, T // 4]))
         w_raw = keep.tile([P, 2 * H], U8, name="w_raw")
         nc.sync.dma_start(w_raw[:].bitcast(I32), w1_words[0].bitcast(I32))
-        cand_t = load_list("cand_t", cand)
         load_w_scales(0)
         load_w_scales(1)
+        load_w_scales(2)
         x_w = keep.tile([P, T], U32, name="x_w")
         nc.sync.dma_start(x_w[:].bitcast(I32), x_words[0].rearrange("p n t -> p (n t)").bitcast(I32))
-        load_w_scales(2)
         load_w_scales(3)
+        cand_t = load_list("cand_t", cand)
         gs_t = keep.tile([P, PACK], F32, name="gs_t")
         nc.sync.dma_start(gs_t[:], gs.rearrange("(p t) o -> p (t o)", t=PACK))
         n1_t = load_list("n1_t", n1)
@@ -97,22 +97,14 @@ def tile_picked_hcandhopnstd_none_po_kernel(
         place_scales(nc.scalar, xq_sc, xq_sc_g)
 
         w_w = keep.tile([P, 2 * H], U8, name="w_w", align_bytes=64)
-        nc.gpsimd.tensor_copy(
+        nc.vector.tensor_copy(
             w_w[:].rearrange("p (t m b) -> p t m b", t=PACK, b=2),
             w_raw[:].rearrange("p (m t b) -> p t m b", t=PACK, b=2),
         )
         w_sc = keep.tile([P, H], U8, name="w_sc", align_bytes=64)
-        nc.gpsimd.tensor_copy(
+        nc.vector.tensor_copy(
             w_sc[:].rearrange("p (t m) -> p t m", t=PACK), w_sc_raw[:].rearrange("p (m t) -> p t m", t=PACK)
         )
-        xc_sc_g = keep.tile([P, C], U8, name="xc_sc_g")
-        nc.vector.tensor_copy(xc_sc_g[:], x_sc[:].indirect(cand_t[:]))
-        xc_sc_d = keep.tile([P, C], U8, name="xc_sc_d")
-        nc.vector.tensor_copy(
-            xc_sc_d[:].rearrange("p (t m) -> p t m", t=PACK), xc_sc_g[:].rearrange("p (m t) -> p t m", t=PACK)
-        )
-        place_scales(nc.sync, xc_sc, xc_sc_d)
-
         xq_w = keep.tile([P, S], U32, name="xq_w", align_bytes=64)
         nc.vector.tensor_copy(xq_w[:], x_w[:].indirect(offs_t[:]))
 
@@ -136,7 +128,7 @@ def tile_picked_hcandhopnstd_none_po_kernel(
         )
 
         def planes(name):
-            return [keep.tile([P, S], F32, name="%s%d" % (name, t)) for t in range(PACK)]
+            return [keep.tile([P, S], F32, name="%s%d" % (name, t), tag="%s%d" % (name, t)) for t in range(PACK)]
 
         y_g, st, mag, root, r = [planes(name) for name in ("y_g", "st", "mag", "root", "r")]
 
@@ -145,7 +137,8 @@ def tile_picked_hcandhopnstd_none_po_kernel(
 
         def differ(t):
             nc.vector.tensor_copy(y_g[t][:], win[t][:].indirect(n1_t[:]))
-            nc.gpsimd.tensor_tensor(st[t][:], win[t][:, :S], y_g[t][:], ALU.subtract)
+            engine = nc.vector if t == 0 else nc.gpsimd
+            engine.tensor_tensor(st[t][:], win[t][:, :S], y_g[t][:], ALU.subtract)
 
         def size(t):
             nc.scalar.activation(mag[t][:], st[t][:], ACT.Abs, scale=g_inv[:, t : t + 1])
@@ -166,36 +159,48 @@ def tile_picked_hcandhopnstd_none_po_kernel(
             inv_root(t)
         square(PACK - 1)
 
+        xc_sc_g = keep.tile([P, C], U8, name="xc_sc_g", tag="y_g1")
+        nc.vector.tensor_copy(xc_sc_g[:], x_sc[:].indirect(cand_t[:]))
+        xc_sc_d = keep.tile([P, C], U8, name="xc_sc_d")
+        nc.vector.tensor_copy(
+            xc_sc_d[:].rearrange("p (t m) -> p t m", t=PACK), xc_sc_g[:].rearrange("p (m t) -> p t m", t=PACK)
+        )
+        place_scales(nc.sync, xc_sc, xc_sc_d)
+
         z_w = keep.tile([P, S], U32, name="z_w", align_bytes=64)
         z_sc = keep.tile([P, S], U8, name="z_sc", align_bytes=64)
         s_ps = [psum.tile([P, S], F32, name="s_ps%d" % t, tag="s%d" % t) for t in range(PACK)]
-        z = [keep.tile([P, PACK, width], F32, name="z%d" % c0) for c0, width in CHUNKS]
-
-        def weigh(chunk, t):
-            c0, width = CHUNKS[chunk]
-            nc.vector.tensor_tensor(
-                z[chunk][:, t, :], r[t][:].indirect(entries(n2_t, c0, width)), st[t][:, c0 : c0 + width], ALU.mult
-            )
-
+        z = [keep.tile([P, PACK, HALF], F32, name="z%d" % c0) for c0 in range(0, S, HALF)]
         for t in range(PACK):
-            for chunk in range(len(CHUNKS)):
-                weigh(chunk, t)
-        z_b = [keep.tile([P, PACK * width], BF16, name="z_b%d" % c0, align_bytes=64) for c0, width in CHUNKS]
-        interleave(nc.scalar.copy, z_b[0][:], z[0][:])
-        interleave(nc.vector.tensor_copy, z_b[1][:], z[1][:])
-        for chunk in (1, 0):
-            cols = slice(CHUNKS[chunk][0], sum(CHUNKS[chunk]))
-            nc.vector.quantize_mx(z_w[:, cols].bitcast(FP8X4), z_sc[:, cols], z_b[chunk][:])
-        for t in range(PACK):
+            width = HALF if t + 1 < PACK else CHUNK
+            for c0 in range(0, S, width):
+                nc.vector.tensor_tensor(
+                    z[c0 // HALF][:, t, c0 % HALF : c0 % HALF + width],
+                    r[t][:].indirect(entries(n2_t, c0, width)),
+                    st[t][:, c0 : c0 + width],
+                    ALU.mult,
+                )
+
+        def score(t, cols):
             nc.tensor.matmul_mx(
-                s_ps[t][:],
+                s_ps[t][:, cols],
                 lhsT=xc_w[:, P * t : P * (t + 1)].bitcast(FP8X4),
                 lhsT_scale=xc_sc[:, P * t : P * (t + 1)],
-                rhs=z_w[:].bitcast(FP8X4),
-                rhs_scale=z_sc[:],
+                rhs=z_w[:, cols].bitcast(FP8X4),
+                rhs_scale=z_sc[:, cols],
                 start=True,
                 stop=True,
             )
+
+        for c0 in range(0, S, CHUNK):
+            cols = slice(c0, c0 + CHUNK)
+            z_c = z[c0 // HALF][:, :, c0 % HALF : c0 % HALF + CHUNK]
+            z_b = keep.tile([P, PACK * CHUNK], BF16, name="z_b%d" % c0, align_bytes=64)
+            interleave(nc.scalar.copy if c0 + CHUNK < S else nc.vector.tensor_copy, z_b[:], z_c)
+            nc.vector.quantize_mx(z_w[:, cols].bitcast(FP8X4), z_sc[:, cols], z_b[:])
+            score(0, cols)
+        for t in range(1, PACK):
+            score(t, slice(0, S))
         nc.scalar.activation(win[0][:, :S], s_ps[0][:], ACT.Copy, scale=0.0625)
 
         o_w = keep.tile([P, S], U32, name="o_w", align_bytes=64)

@@ -22,6 +22,7 @@ PACK = 4
 LANES = 16
 HALF = 256
 CHUNK = 128
+PLAIN = 2
 
 
 def tile_picked_hcandhopnstd_none_po_kernel(
@@ -134,11 +135,15 @@ def tile_picked_hcandhopnstd_none_po_kernel(
 
         def leave(t):
             nc.scalar.activation(win[t][:, :S], y_ps[t][:], ACT.Copy, scale=gs_t[:, t : t + 1])
+            if t >= PLAIN:
+                nc.scalar.activation(y_g[t][:], y_ps[t][:], ACT.Copy, scale=gs_t[:, t : t + 1])
 
         def differ(t):
-            nc.vector.tensor_copy(y_g[t][:], win[t][:].indirect(n1_t[:]))
-            engine = nc.vector if t == 0 else nc.gpsimd
-            engine.tensor_tensor(st[t][:], win[t][:, :S], y_g[t][:], ALU.subtract)
+            if t < PLAIN:
+                nc.vector.tensor_copy(y_g[t][:], win[t][:].indirect(n1_t[:]))
+                nc.vector.tensor_tensor(st[t][:], y_g[t][:], win[t][:, :S], ALU.subtract)
+            else:
+                nc.vector.tensor_tensor(st[t][:], win[t][:].indirect(n1_t[:]), y_g[t][:], ALU.subtract)
 
         def size(t):
             nc.scalar.activation(mag[t][:], st[t][:], ACT.Abs, scale=g_inv[:, t : t + 1])
@@ -201,7 +206,7 @@ def tile_picked_hcandhopnstd_none_po_kernel(
             score(0, cols)
         for t in range(1, PACK):
             score(t, slice(0, S))
-        nc.scalar.activation(win[0][:, :S], s_ps[0][:], ACT.Copy, scale=0.0625)
+        nc.scalar.activation(win[0][:, :S], s_ps[0][:], ACT.Copy, scale=-0.0625)
 
         o_w = keep.tile([P, S], U32, name="o_w", align_bytes=64)
         o_sc = keep.tile([P, S], U8, name="o_sc", align_bytes=64)
@@ -229,8 +234,8 @@ def tile_picked_hcandhopnstd_none_po_kernel(
 
         for t in range(PACK):
             if t + 1 < PACK:
-                nc.scalar.activation(win[t + 1][:, :S], s_ps[t + 1][:], ACT.Copy, scale=0.0625)
-            nc.scalar.activation(s3[t][:], s_ps[t][:], ACT.Copy, scale=-5.0 / 48.0)
+                nc.scalar.activation(win[t + 1][:, :S], s_ps[t + 1][:], ACT.Copy, scale=-0.0625)
+            nc.scalar.activation(s3[t][:], s_ps[t][:], ACT.Copy, scale=5.0 / 48.0)
             nc.vector.tensor_copy(pa[t][:], win[t][:].indirect(n3_t[:]))
             nc.vector.tensor_tensor(v[t][:], win[t][:].indirect(n4_t[:]), pa[t][:], ALU.subtract)
             nc.vector.scalar_tensor_tensor(u[t][:], pa[t][:], 2.0, v[t][:], ALU.mult, ALU.add)

from contextlib import ExitStack

import concourse.mybir as mybir
from concourse.masks import make_identity

K, T, S, H, C = 512, 2048, 512, 512, 512
FLOPS = 2 * K * H * S + 2 * K * C * S

F32 = mybir.dt.float32
BF16 = mybir.dt.bfloat16
I32 = mybir.dt.int32
U32 = mybir.dt.uint32
U16 = mybir.dt.uint16
U8 = mybir.dt.uint8
FP8X4 = mybir.dt.float8_e4m3fn_x4
FP4X4 = mybir.dt.float4_e2m1fn_x4
ALU = mybir.AluOpType
ACT = mybir.ActivationFunctionType

P = 128
PACK = 4
LANES = 16
HALF = 256
CHUNK = 128
PLAIN = 2


def tile_picked_hcandhopnstd_none_po_kernel(
    tc, x_words, x_scales, w1_words, w1_scales, gs, offs, n1, n2, cand, n3, n4, out_0, out_1, out_2
):
    nc = tc.nc
    with ExitStack() as ctx:
        keep = ctx.enter_context(tc.tile_pool(name="keep", bufs=1))
        psum = ctx.enter_context(tc.psum_pool(name="psum", bufs=1))

        def load_list(name, dram):
            tile = keep.tile([P, S // LANES], U16, name=name)
            nc.sync.dma_start(tile[:], dram)
            return tile

        def entries(lst, c0, width):
            return lst[:, c0 // LANES : (c0 + width) // LANES]

        def interleave(copy, dst, src):
            copy(
                dst.rearrange("p (c i t) -> p c t i", i=4, t=PACK),
                src.rearrange("p t (c i) -> p c t i", i=4),
            )

        x_sc = keep.tile([P, T], U8, name="x_sc")
        w_sc_raw = keep.tile([P, H], U8, name="w_sc_raw")

        def load_w_scales(q):
            rows = w1_scales[0, 4 * q : 4 * q + 4, :].bitcast(I32)
            nc.sync.dma_start(w_sc_raw[32 * q : 32 * q + 32, :].bitcast(I32), rows.unsqueeze(0).to_broadcast([8, 4, H // 4]))

        offs_t = load_list("offs_t", offs)
        nc.sync.dma_start(x_sc[:].bitcast(I32), x_scales[0].bitcast(I32).unsqueeze(1).to_broadcast([16, 8, T // 4]))
        w_raw = keep.tile([P, 2 * H], U8, name="w_raw")
        nc.sync.dma_start(w_raw[:].bitcast(I32), w1_words[0].bitcast(I32))
        load_w_scales(0)
        load_w_scales(1)
        load_w_scales(2)
        x_w = keep.tile([P, T], U32, name="x_w")
        nc.sync.dma_start(x_w[:].bitcast(I32), x_words[0].rearrange("p n t -> p (n t)").bitcast(I32))
        load_w_scales(3)
        cand_t = load_list("cand_t", cand)
        gs_t = keep.tile([P, PACK], F32, name="gs_t")
        nc.sync.dma_start(gs_t[:], gs.rearrange("(p t) o -> p (t o)", t=PACK))
        n1_t = load_list("n1_t", n1)
        n2_t = load_list("n2_t", n2)
        n3_t = load_list("n3_t", n3)
        n4_t = load_list("n4_t", n4)

        warm = keep.tile([P, 1], F32, name="warm")
        nc.vector.memset(warm[:], 1.0)
        nc.scalar.activation(warm[:], warm[:], ACT.Abs_reciprocal_sqrt)
        xq_sc = keep.tile([P, S], U8, name="xq_sc", align_bytes=64)
        xc_sc = keep.tile([P, C], U8, name="xc_sc", align_bytes=64)
        nc.gpsimd.memset(xq_sc[:].bitcast(I32), 0)
        nc.gpsimd.memset(xc_sc[:].bitcast(I32), 0)
        win = [keep.tile([P, 2 * S], F32, name="win%d" % t) for t in range(PACK)]
        for t in range(PACK):
            nc.gpsimd.memset(win[t][:, S:], 0.0)
        ident = keep.tile([P, P], F32, name="ident")
        make_identity(nc, ident[:])
        g_abs = keep.tile([P, PACK], F32, name="g_abs")
        g_inv = keep.tile([P, PACK], F32, name="g_inv")
        nc.scalar.activation(g_abs[:], gs_t[:], ACT.Abs_reciprocal_sqrt, bias=1e-30)
        nc.scalar.activation(g_inv[:], g_abs[:], ACT.Square)

        def place_scales(queue, dst, src):
            for q in range(4):
                queue.dma_start(dst[32 * q : 32 * q + 4, :].bitcast(I32), src[32 * q : 32 * q + 32 : 8, :].bitcast(I32))

        xq_sc_g = keep.tile([P, S], U8, name="xq_sc_g")
        nc.vector.tensor_copy(xq_sc_g[:], x_sc[:].indirect(offs_t[:]))
        place_scales(nc.scalar, xq_sc, xq_sc_g)

        w_w = keep.tile([P, 2 * H], U8, name="w_w", align_bytes=64)
        nc.vector.tensor_copy(
            w_w[:].rearrange("p (t m b) -> p t m b", t=PACK, b=2),
            w_raw[:].rearrange("p (m t b) -> p t m b", t=PACK, b=2),
        )
        w_sc = keep.tile([P, H], U8, name="w_sc", align_bytes=64)
        nc.vector.tensor_copy(
            w_sc[:].rearrange("p (t m) -> p t m", t=PACK), w_sc_raw[:].rearrange("p (m t) -> p t m", t=PACK)
        )
        xq_w = keep.tile([P, S], U32, name="xq_w", align_bytes=64)
        nc.vector.tensor_copy(xq_w[:], x_w[:].indirect(offs_t[:]))

        y_ps = [psum.tile([P, S], F32, name="y_ps%d" % t, tag="y%d" % t) for t in range(PACK)]
        for t in range(PACK):
            nc.tensor.matmul_mx(
                y_ps[t][:],
                lhsT=w_w[:, 2 * P * t : 2 * P * (t + 1)].bitcast(FP4X4),
                lhsT_scale=w_sc[:, P * t : P * (t + 1)],
                rhs=xq_w[:].bitcast(FP8X4),
                rhs_scale=xq_sc[:],
                start=True,
                stop=True,
            )

        xc_w_g = keep.tile([P, C], U32, name="xc_w_g")
        nc.vector.tensor_copy(xc_w_g[:], x_w[:].indirect(cand_t[:]))
        xc_w = keep.tile([P, C], U32, name="xc_w", align_bytes=64)
        nc.vector.tensor_copy(
            xc_w[:].rearrange("p (t m) -> p t m", t=PACK), xc_w_g[:].rearrange("p (m t) -> p t m", t=PACK)
        )

        def planes(name):
            return [keep.tile([P, S], F32, name="%s%d" % (name, t), tag="%s%d" % (name, t)) for t in range(PACK)]

        y_g, st, mag, root, r = [planes(name) for name in ("y_g", "st", "mag", "root", "r")]

        def leave(t):
            nc.scalar.activation(win[t][:, :S], y_ps[t][:], ACT.Copy, scale=gs_t[:, t : t + 1])
            if t >= PLAIN:
                nc.scalar.activation(y_g[t][:], y_ps[t][:], ACT.Copy, scale=gs_t[:, t : t + 1])

        def differ(t):
            if t < PLAIN:
                nc.vector.tensor_copy(y_g[t][:], win[t][:].indirect(n1_t[:]))
                nc.vector.tensor_tensor(st[t][:], y_g[t][:], win[t][:, :S], ALU.subtract)
            else:
                nc.vector.tensor_tensor(st[t][:], win[t][:].indirect(n1_t[:]), y_g[t][:], ALU.subtract)

        def size(t):
            nc.scalar.activation(mag[t][:], st[t][:], ACT.Abs, scale=g_inv[:, t : t + 1])

        def inv_root(t):
            nc.scalar.activation(root[t][:], mag[t][:], ACT.Abs_reciprocal_sqrt, bias=0.5)

        def square(t):
            nc.scalar.activation(r[t][:], root[t][:], ACT.Square)

        for t in range(PACK):
            leave(t)
        for t in range(PACK):
            differ(t)
            size(t)
            if t > 0:
                square(t - 1)
            inv_root(t)
        square(PACK - 1)

        xc_sc_g = keep.tile([P, C], U8, name="xc_sc_g", tag="y_g1")
        nc.vector.tensor_copy(xc_sc_g[:], x_sc[:].indirect(cand_t[:]))
        xc_sc_d = keep.tile([P, C], U8, name="xc_sc_d")
        nc.vector.tensor_copy(
            xc_sc_d[:].rearrange("p (t m) -> p t m", t=PACK), xc_sc_g[:].rearrange("p (m t) -> p t m", t=PACK)
        )
        place_scales(nc.sync, xc_sc, xc_sc_d)

        z_w = keep.tile([P, S], U32, name="z_w", align_bytes=64)
        z_sc = keep.tile([P, S], U8, name="z_sc", align_bytes=64)
        s_ps = [psum.tile([P, S], F32, name="s_ps%d" % t, tag="s%d" % t) for t in range(PACK)]
        z = [keep.tile([P, PACK, HALF], F32, name="z%d" % c0) for c0 in range(0, S, HALF)]
        for t in range(PACK):
            width = HALF if t + 1 < PACK else CHUNK
            for c0 in range(0, S, width):
                nc.vector.tensor_tensor(
                    z[c0 // HALF][:, t, c0 % HALF : c0 % HALF + width],
                    r[t][:].indirect(entries(n2_t, c0, width)),
                    st[t][:, c0 : c0 + width],
                    ALU.mult,
                )

        def score(t, cols):
            nc.tensor.matmul_mx(
                s_ps[t][:, cols],
                lhsT=xc_w[:, P * t : P * (t + 1)].bitcast(FP8X4),
                lhsT_scale=xc_sc[:, P * t : P * (t + 1)],
                rhs=z_w[:, cols].bitcast(FP8X4),
                rhs_scale=z_sc[:, cols],
                start=True,
                stop=True,
            )

        for c0 in range(0, S, CHUNK):
            cols = slice(c0, c0 + CHUNK)
            z_c = z[c0 // HALF][:, :, c0 % HALF : c0 % HALF + CHUNK]
            z_b = keep.tile([P, PACK * CHUNK], BF16, name="z_b%d" % c0, align_bytes=64)
            interleave(nc.scalar.copy if c0 + CHUNK < S else nc.vector.tensor_copy, z_b[:], z_c)
            nc.vector.quantize_mx(z_w[:, cols].bitcast(FP8X4), z_sc[:, cols], z_b[:])
            score(0, cols)
        for t in range(1, PACK):
            score(t, slice(0, S))
        nc.scalar.activation(win[0][:, :S], s_ps[0][:], ACT.Copy, scale=-0.0625)

        o_w = keep.tile([P, S], U32, name="o_w", align_bytes=64)
        o_sc = keep.tile([P, S], U8, name="o_sc", align_bytes=64)
        out_rows = out_0.rearrange("(p t) c -> p t c", t=PACK)
        out_words = out_1[0].rearrange("p n t -> p (n t)").bitcast(I32)
        o = keep.tile([P, PACK, S], F32, name="o")
        pa, u, v, s3, num, v2, w2, rs = [planes(name) for name in ("pa", "u", "v", "s3", "num", "v2", "w2", "rs")]

        def turned_sum(bank, terms):
            for c0 in range(0, S, P):
                for i, term in enumerate(terms):
                    nc.tensor.matmul(
                        bank[:, c0 : c0 + P],
                        term[:, c0 : c0 + P],
                        ident[:],
                        start=(i == 0),
                        stop=(i == len(terms) - 1),
                        is_transpose=True,
                    )

        def spread(t):
            q_ps = psum.tile([P, S], F32, name="q_ps%d" % t, tag="y%d" % ((t + 1) % PACK))
            turned_sum(q_ps, (v2[t], w2[t]))
            nc.scalar.activation(rs[t][:], q_ps[:], ACT.Abs_reciprocal_sqrt, scale=0.5, bias=0.25)

        for t in range(PACK):
            if t + 1 < PACK:
                nc.scalar.activation(win[t + 1][:, :S], s_ps[t + 1][:], ACT.Copy, scale=-0.0625)
            nc.scalar.activation(s3[t][:], s_ps[t][:], ACT.Copy, scale=5.0 / 48.0)
            nc.vector.tensor_copy(pa[t][:], win[t][:].indirect(n3_t[:]))
            nc.vector.tensor_tensor(v[t][:], win[t][:].indirect(n4_t[:]), pa[t][:], ALU.subtract)
            nc.vector.scalar_tensor_tensor(u[t][:], pa[t][:], 2.0, v[t][:], ALU.mult, ALU.add)
            v_ps = psum.tile([P, S], F32, name="v_ps%d" % t, tag="y%d" % t)
            turned_sum(v_ps, (v[t],))
            nc.scalar.activation(v2[t][:], v_ps[:], ACT.Square)
            w_ps = psum.tile([P, S], F32, name="w_ps%d" % t, tag="s%d" % t)
            turned_sum(w_ps, (s3[t], u[t]))
            nc.scalar.activation(w2[t][:], w_ps[:], ACT.Square, scale=0.375)
            if t > 0:
                spread(t - 1)
        spread(PACK - 1)

        for t in range(PACK):
            nc.vector.scalar_tensor_tensor(num[t][:], win[t][:, :S], 2.2, u[t][:], ALU.mult, ALU.subtract)
        last = PACK - 1
        for t in range(last):
            nc.vector.scalar_tensor_tensor(o[:, t, :], num[t][:], 0.3125, rs[t][:], ALU.mult, ALU.mult)
            nc.sync.dma_start(out_rows[:, t, :], o[:, t, :])
        halves = ((0, nc.scalar.copy), (HALF, nc.vector.tensor_copy))
        for c0, copy in halves:
            cols = slice(c0, c0 + HALF)
            nc.vector.scalar_tensor_tensor(o[:, last, cols], num[last][:, cols], 0.3125, rs[last][:, cols], ALU.mult, ALU.mult)
        nc.sync.dma_start(out_rows[:, last, :], o[:, last, :])
        for c0, copy in reversed(halves):
            cols = slice(c0, c0 + HALF)
            o_b = keep.tile([P, PACK * HALF], BF16, name="o_b%d" % c0, align_bytes=64)
            interleave(copy, o_b[:], o[:, :, cols])
            nc.vector.quantize_mx(o_w[:, cols].bitcast(FP8X4), o_sc[:, cols], o_b[:])
            nc.sync.dma_start(out_words[:, cols], o_w[:, cols].bitcast(I32))
        for q in range(4):
            nc.scalar.dma_start(out_2[0, 4 * q : 4 * q + 4, :].bitcast(I32), o_sc[32 * q : 32 * q + 4, :].bitcast(I32))
